import numpy as np
import ml_dtypes


def mxq(x, axis, fmt="e4m3"):
    dtype, down = {"e4m3": (ml_dtypes.float8_e4m3fn, 7), "e5m2": (ml_dtypes.float8_e5m2, 14)}[fmt]
    v = np.moveaxis(np.asarray(x, np.float32).astype(ml_dtypes.bfloat16).astype(np.float64), axis, -1)
    blocks = v.reshape(v.shape[:-1] + (-1, 32))
    amax = np.abs(blocks).max(-1, keepdims=True)
    byte = np.maximum(np.where(amax > 0, np.frexp(amax)[1] - 1 + 127, 0) - down, 1)
    scale = np.exp2(byte - 127.0)
    codes = (blocks / scale).astype(np.float32).astype(dtype).astype(np.float64)
    return np.moveaxis((codes * scale).reshape(v.shape), -1, axis)


WIDE = False


def mx_kscale(k):
    if not WIDE:
        return np.ones(k)
    levels = np.array([10, -10, 5, -5, 0])
    if k % 512:
        return np.exp2(np.random.permutation(np.resize(levels, k // 32))).repeat(32)
    a = np.empty((k // 512, 16))
    for p in range(k // 512):
        a[p, :8] = np.random.permutation(np.resize(levels, 8))
        for g in range(8):
            far = levels[np.abs(levels - a[p, g]) >= 10]
            a[p, g + 8] = far[np.random.randint(len(far))]
    return np.exp2(a.ravel()).repeat(32)


def f64(x):
    return np.asarray(x).astype(np.float64)


def striped(idx):
    return np.tile(np.asarray(idx).reshape(-1, 16).T, (8, 1)).astype(np.uint16)


def unstriped(offs):
    return offs[:16].T.reshape(-1).astype(np.int64)


def striped8(idx):
    return np.asarray(idx).reshape(8, -1, 16).transpose(0, 2, 1).reshape(128, -1).astype(np.uint16)


def unstriped8(offs):
    return offs.reshape(8, 16, -1).transpose(0, 2, 1).reshape(8, -1).astype(np.int64)


def pick8(x, idx, run):
    r = np.arange(len(x))
    return x[r[:, None], idx[r % (8 * run) // run]]


E2M1 = np.array([0.0, 0.5, 1.0, 1.5, 2.0, 3.0, 4.0, 6.0, -0.0, -0.5, -1.0, -1.5, -2.0, -3.0, -4.0, -6.0])


def pack_weight(w, fmt):
    k, n = w.shape
    w = f64(np.asarray(w, np.float32).astype(ml_dtypes.bfloat16)).reshape(k // 32, 32, n)
    amax = np.abs(w).max(1)
    if fmt == "e4m3":
        byte = np.frexp(amax)[1] - 1 + 127 - 7
    else:
        mant, ex = np.frexp(amax / 6.0)
        byte = np.where(mant > 0.5, ex, ex - 1) + 127
    byte = np.clip(np.where(amax > 0, byte, 1), 1, 254)
    scaled = (w * np.exp2(127.0 - byte)[:, None, :]).reshape(k, n).astype(np.float32)
    by_word = np.ascontiguousarray(scaled.reshape(k // 512, 128, 4, n).transpose(0, 1, 3, 2))
    if fmt == "e4m3":
        words = by_word.astype(ml_dtypes.float8_e4m3fn).view(np.uint8)
    else:
        c = by_word.astype(ml_dtypes.float4_e2m1fn).view(np.uint8) & 0xF
        words = (c[..., 0::2] | (c[..., 1::2] << 4)).reshape(k // 512, 128, 2 * n)
    return np.ascontiguousarray(words), np.ascontiguousarray(byte.astype(np.uint8).reshape(k // 512, 16, n))


def unpack_weight(words, scales, fmt):
    g, _, n = scales.shape
    words = np.ascontiguousarray(words).reshape(g, 128, n, -1)
    if fmt == "e4m3":
        vals = words.view(ml_dtypes.float8_e4m3fn).astype(np.float64)
    else:
        nib = np.empty((g, 128, n, 4), np.uint8)
        nib[..., 0::2] = words & 0xF
        nib[..., 1::2] = words >> 4
        vals = E2M1[nib]
    vals = vals * np.repeat(np.exp2(scales.astype(np.float64) - 127.0), 8, axis=1)[..., None]
    return vals.transpose(0, 1, 3, 2).reshape(g * 512, n)


K, J, R, T, U, F, G, O, D, N, S = 512, 256, 512, 512, 512, 2048, 1024, 128, 512, 256, 1024


def setup_inputs():
    n = np.random.standard_normal
    idx = np.stack([np.random.permutation(T)[:J] for _ in range(8)])
    idx2 = np.stack([np.random.permutation(U)[:J] for _ in range(8)])
    idx3 = np.stack([np.random.permutation(F)[:G] for _ in range(8)])
    idx4 = np.random.permutation(G)[:R]
    idx5 = np.stack([np.random.permutation(J)[:O] for _ in range(8)])
    idx6 = np.stack([np.random.permutation(D)[:O] for _ in range(8)])
    idx7 = np.random.permutation(S)[:N]
    fk = mx_kscale(K)
    fr = mx_kscale(R)
    vsp = pack_weight(n((R, S)) * 1 / np.sqrt(R) / fr[:, None], "e2m1")
    return {
        "ta": (np.random.randint(-7, 8, (K, T)).astype(np.float64)).astype(np.float32),
        "tb": (np.random.randint(-7, 8, (K, U)).astype(np.float64)).astype(np.float32),
        "ga": ((np.random.randint(8, 25, (K, 1)) / 64.0) * fk[:, None]).astype(np.float32),
        "gb": ((np.random.randint(8, 25, (K, 1)) / 64.0) * fk[:, None]).astype(np.float32),
        "ua": (np.random.randint(-7, 8, (K, F)).astype(np.float64)).astype(np.float32),
        "ha": ((np.random.randint(8, 25, (K, 1)) / 1024.0) / fk[:, None]).astype(np.float32),
        "hb": (np.random.uniform(0.5, 1.6, (K, 1))).astype(np.float32),
        "tl": (np.random.randint(1, 9, (R, D)).astype(np.float64)).astype(np.float32),
        "sa": (np.random.uniform(0.5, 1.6, (R, 1)) * fr[:, None]).astype(np.float32),
        "sl": (np.random.uniform(0.1, 0.4, (R, 1))).astype(np.float32),
        "vs_words": vsp[0],
        "vs_scales": vsp[1],
        "offs": striped8(idx),
        "offs2": striped8(idx2),
        "offs3": striped8(idx3),
        "offs4": striped(idx4),
        "offs5": striped8(idx5),
        "offs6": striped8(idx6),
        "offs7": striped(idx7),
    }


def reference(ta, tb, ga, gb, ua, ha, hb, tl, sa, sl, vs_words, vs_scales, offs, offs2, offs3, offs4, offs5, offs6, offs7):
    idx = unstriped8(offs)
    idx2 = unstriped8(offs2)
    idx3 = unstriped8(offs3)
    idx4 = unstriped(offs4)
    idx5 = unstriped8(offs5)
    idx6 = unstriped8(offs6)
    idx7 = unstriped(offs7)
    vsu = unpack_weight(vs_words, vs_scales, "e2m1")
    xc = np.maximum(pick8(f64(ta), idx, 64) * f64(ga), pick8(f64(tb), idx2, 64) * f64(gb))
    wcd = pick8(f64(ua), idx3, 64) * f64(ha)
    wc = wcd[:, idx4] * f64(hb)
    wcq = mxq(wc, 0, "e4m3")
    xcq = mxq(xc, 0, "e4m3")
    a = wcq.T @ xcq
    hid = pick8(a, idx5, 64) * f64(sa) * pick8(f64(tl), idx6, 64) * f64(sl)
    vsidx7g = vsu[:, idx7]
    hidq = mxq(hid, 0, "e4m3")
    y = vsidx7g.T @ hidq
    return y

@@ -1,0 +1,195 @@
+from contextlib import ExitStack
+
+import concourse.mybir as mybir
+
+K, J, R, T, U, F, G, O, D, N, S = 512, 256, 512, 512, 512, 2048, 1024, 128, 512, 256, 1024
+FLOPS = 2 * K * R * J + 2 * R * N * O
+
+F32 = mybir.dt.float32
+BF16 = mybir.dt.bfloat16
+I32 = mybir.dt.int32
+U32 = mybir.dt.uint32
+U16 = mybir.dt.uint16
+U8 = mybir.dt.uint8
+FP8X4 = mybir.dt.float8_e4m3fn_x4
+FP4X4 = mybir.dt.float4_e2m1fn_x4
+COPY = mybir.ActivationFunctionType.Copy
+ALU = mybir.AluOpType
+
+P = 128
+PACK = 4
+HALF = J // 2
+RUN = 4
+
+
+def plane(table, t):
+    return table.rearrange("(p t) c -> p t c", t=PACK)[:, t, :]
+
+
+def by_plane(column):
+    return column.rearrange("(p t) one -> p (t one)", t=PACK)
+
+
+def tile_picked_largercode_respelled_one_codedgain_store_plain_kernel(
+    tc, ta, tb, ga, gb, ua, ha, hb, tl, sa, sl, vs_words, vs_scales,
+    offs, offs2, offs3, offs4, offs5, offs6, offs7, out,
+):
+    nc = tc.nc
+    with ExitStack() as ctx:
+        sb = ctx.enter_context(tc.tile_pool(name="sb", bufs=1))
+        ps = ctx.enter_context(tc.psum_pool(name="ps", bufs=1))
+
+        def load_list(src, name):
+            dst = sb.tile(list(src.shape), U16, name=name)
+            nc.sync.dma_start(dst[:], src)
+            return dst
+
+        def load_plane(table, t, name):
+            dst = sb.tile([P, table.shape[1]], F32, name="%s%d" % (name, t))
+            nc.sync.dma_start(dst[:], plane(table, t))
+            return dst
+
+        def load_factors(engine, src, name):
+            dst = sb.tile(list(src.shape), F32, name=name)
+            engine.dma_start(dst[:], src)
+            return dst
+
+        def gather_scaled(dst, window, offsets, factor):
+            nc.scalar.activation(out=dst, in_=window[:].indirect(offsets), func=COPY, scale=factor)
+
+        ha_sb = load_factors(nc.scalar, by_plane(ha), "ha_sb")
+        ua_sb = [load_plane(ua, 0, "ua")]
+        l3 = load_list(offs3, "l3")
+        ua_sb.append(load_plane(ua, 1, "ua"))
+        l4 = load_list(offs4, "l4")
+        hb_early = load_factors(nc.sync, by_plane(hb)[:, 0:2], "hb_early")
+        ga_sb = load_factors(nc.sync, by_plane(ga), "ga_sb")
+        gb_sb = load_factors(nc.sync, by_plane(gb), "gb_sb")
+        ua_sb.append(load_plane(ua, 2, "ua"))
+        ua_sb.append(load_plane(ua, 3, "ua"))
+        hb_late = load_factors(nc.sync, by_plane(hb)[:, 2:4], "hb_late")
+        l7 = load_list(offs7, "l7")
+        words = sb.tile([P, 2 * S], U8, name="words")
+        nc.sync.dma_start(words[:].bitcast(I32), vs_words[0].bitcast(I32))
+        ta_sb, tb_sb = [], []
+        for t in range(PACK):
+            ta_sb.append(load_plane(ta, t, "ta"))
+            tb_sb.append(load_plane(tb, t, "tb"))
+        l1 = load_list(offs, "l1")
+        l2 = load_list(offs2, "l2")
+        l6 = load_list(offs6, "l6")
+        tl_sb = [load_plane(tl, t, "tl") for t in range(PACK)]
+        l5 = load_list(offs5, "l5")
+
+        sl_sb = load_factors(nc.gpsimd, by_plane(sl), "sl_sb")
+        sa_sb = load_factors(nc.gpsimd, by_plane(sa), "sa_sb")
+        scale_rows = sb.tile([P, S], U8, name="scale_rows")
+        nc.vector.memset(scale_rows[:].bitcast(I32), 0)
+        for q in range(4):
+            nc.gpsimd.dma_start(
+                scale_rows[32 * q : 32 * q + 4, :].bitcast(I32),
+                vs_scales[0, 4 * q : 4 * q + 4, :].bitcast(I32),
+            )
+
+        wc = sb.tile([P, PACK, R], BF16, name="wc")
+        for pair, hb_sb in enumerate((hb_early, hb_late)):
+            wcd = []
+            for u in range(2):
+                t = 2 * pair + u
+                wcd.append(sb.tile([P, G], F32, name="wcd%d" % t))
+                gather_scaled(wcd[u][:], ua_sb[t], l3[:], ha_sb[:, t : t + 1])
+            for u in range(2):
+                gather_scaled(wc[:, 2 * pair + u, :], wcd[u], l4[:], hb_sb[:, u : u + 1])
+        wc_grouped = sb.tile([P, R, PACK], BF16, name="wc_grouped", align_bytes=64)
+        nc.vector.tensor_copy(
+            out=wc_grouped[:].rearrange("p (s m e) t -> p m t e s", s=PACK, e=2),
+            in_=wc[:].rearrange("p t (m e s) -> p m t e s", s=PACK, e=2),
+        )
+        wc_codes = sb.tile([P, R], U32, name="wc_codes", align_bytes=64)
+        wc_scales = sb.tile([P, R], U8, name="wc_scales", align_bytes=64)
+        nc.vector.quantize_mx(
+            out=wc_codes[:].bitcast(FP8X4), scales=wc_scales[:],
+            in_=wc_grouped[:].rearrange("p r t -> p (r t)"),
+        )
+
+        vs_codes = sb.tile([P, 2 * N], U8, name="vs_codes", align_bytes=64)
+        vs_bytes = sb.tile([P, N], U8, name="vs_bytes", align_bytes=64)
+        nc.vector.tensor_copy(out=vs_codes[:].bitcast(U16), in_=words[:].bitcast(U16).indirect(l7[:]))
+        nc.vector.tensor_copy(out=vs_bytes[:], in_=scale_rows[:].indirect(l7[:]))
+
+        a_sb = [sb.tile([P, J], F32, name="a%d" % s) for s in range(PACK)]
+        first_bank = ps.tile([P, PACK, HALF], F32, name="first_bank")
+        sums = []
+        for h in range(2):
+            cols = slice(h * HALF // 16, (h + 1) * HALF // 16)
+            xa = sb.tile([P, PACK, HALF], F32, name="xa%d" % h)
+            xb = sb.tile([P, PACK, HALF], F32, name="xb%d" % h)
+            for t in range(PACK):
+                gather_scaled(xa[:, t, :], ta_sb[t], l1[:, cols], ga_sb[:, t : t + 1])
+                gather_scaled(xb[:, t, :], tb_sb[t], l2[:, cols], gb_sb[:, t : t + 1])
+            xc_grouped = sb.tile([P, HALF, PACK], BF16, name="xc_grouped%d" % h, align_bytes=64)
+            nc.vector.tensor_tensor(
+                out=xc_grouped[:].rearrange("p (c i) t -> p c t i", i=RUN),
+                in0=xa[:].rearrange("p t (c i) -> p c t i", i=RUN),
+                in1=xb[:].rearrange("p t (c i) -> p c t i", i=RUN),
+                op=ALU.max,
+            )
+            xc_codes = sb.tile([P, HALF], U32, name="xc_codes%d" % h, align_bytes=64)
+            xc_scales = sb.tile([P, HALF], U8, name="xc_scales%d" % h, align_bytes=64)
+            nc.vector.quantize_mx(
+                out=xc_codes[:].bitcast(FP8X4), scales=xc_scales[:],
+                in_=xc_grouped[:].rearrange("p j t -> p (j t)"),
+            )
+            for s in range(PACK):
+                if h == 0:
+                    acc = first_bank[:, s, :]
+                else:
+                    bank = ps.tile([P, HALF], F32, name="bank%d" % s)
+                    acc = bank[:]
+                rows = slice(s * P, (s + 1) * P)
+                nc.tensor.matmul_mx(
+                    out=acc,
+                    lhsT=wc_codes[:, rows].bitcast(FP8X4), lhsT_scale=wc_scales[:, rows],
+                    rhs=xc_codes[:].bitcast(FP8X4), rhs_scale=xc_scales[:],
+                    start=True, stop=True,
+                )
+                sums.append((a_sb[s][:, h * HALF : (h + 1) * HALF], acc))
+        for dst, acc in sums:
+            nc.vector.tensor_copy(out=dst, in_=acc)
+
+        gain = sb.tile([P, PACK, O], F32, name="gain")
+        picked = sb.tile([P, PACK, O], F32, name="picked")
+        for s in range(PACK):
+            gather_scaled(gain[:, s, :], tl_sb[s], l6[:], sl_sb[:, s : s + 1])
+        for s in range(PACK):
+            gather_scaled(picked[:, s, :], a_sb[s], l5[:], sa_sb[:, s : s + 1])
+        hid_grouped = sb.tile([P, O, PACK], BF16, name="hid_grouped", align_bytes=64)
+        nc.vector.tensor_tensor(
+            out=hid_grouped[:].rearrange("p (c i) s -> p c s i", i=RUN),
+            in0=picked[:].rearrange("p s (c i) -> p c s i", i=RUN),
+            in1=gain[:].rearrange("p s (c i) -> p c s i", i=RUN),
+            op=ALU.mult,
+        )
+        hid_codes = sb.tile([P, O], U32, name="hid_codes", align_bytes=64)
+        hid_scales = sb.tile([P, O], U8, name="hid_scales", align_bytes=64)
+        nc.vector.quantize_mx(
+            out=hid_codes[:].bitcast(FP8X4), scales=hid_scales[:],
+            in_=hid_grouped[:].rearrange("p o s -> p (o s)"),
+        )
+
+        for b in range(N // P):
+            y_bank = ps.tile([P, O], F32, name="y_bank%d" % b)
+            nc.tensor.matmul_mx(
+                out=y_bank[:],
+                lhsT=vs_codes[:, 2 * P * b : 2 * P * (b + 1)].bitcast(FP4X4),
+                lhsT_scale=vs_bytes[:, P * b : P * (b + 1)],
+                rhs=hid_codes[:].bitcast(FP8X4), rhs_scale=hid_scales[:],
+                start=True, stop=True,
+            )
+            y_sb = sb.tile([P, O], F32, name="y_sb%d" % b)
+            if b == 0:
+                nc.vector.tensor_copy(out=y_sb[:], in_=y_bank[:])
+                nc.sync.dma_start(out[0:P, :], y_sb[:])
+            else:
+                nc.scalar.copy(out=y_sb[:], in_=y_bank[:])
+                nc.scalar.dma_start(out[P : 2 * P, :], y_sb[:])

@@ -19,7 +19,7 @@ ALU = mybir.AluOpType
 P = 128
 PACK = 4
 HALF = J // 2
-RUN = 4
+RUN = 2
 
 
 def plane(table, t):
@@ -102,8 +102,8 @@ def tile_picked_largercode_respelled_one_codedgain_store_plain_kernel(
                 gather_scaled(wc[:, 2 * pair + u, :], wcd[u], l4[:], hb_sb[:, u : u + 1])
         wc_grouped = sb.tile([P, R, PACK], BF16, name="wc_grouped", align_bytes=64)
         nc.vector.tensor_copy(
-            out=wc_grouped[:].rearrange("p (s m e) t -> p m t e s", s=PACK, e=2),
-            in_=wc[:].rearrange("p t (m e s) -> p m t e s", s=PACK, e=2),
+            out=wc_grouped[:].rearrange("p (s m) t -> p s m t", s=PACK),
+            in_=wc[:].rearrange("p t (m s) -> p s m t", s=PACK),
         )
         wc_codes = sb.tile([P, R], U32, name="wc_codes", align_bytes=64)
         wc_scales = sb.tile([P, R], U8, name="wc_scales", align_bytes=64)

@@ -58,6 +58,10 @@ def tile_picked_largercode_respelled_one_codedgain_store_plain_kernel(
             nc.scalar.activation(out=dst, in_=window[:].indirect(offsets), func=COPY, scale=factor)
 
         ha_sb = load_factors(nc.scalar, by_plane(ha), "ha_sb")
+        warm_in = sb.tile([P, 1], F32, name="warm_in")
+        warm_out = sb.tile([P, 1], F32, name="warm_out")
+        nc.vector.memset(warm_in[:], 0.0)
+        nc.scalar.activation(out=warm_out[:], in_=warm_in[:], func=COPY)
         ua_sb = [load_plane(ua, 0, "ua")]
         l3 = load_list(offs3, "l3")
         ua_sb.append(load_plane(ua, 1, "ua"))

@@ -20,6 +20,7 @@ P = 128
 PACK = 4
 HALF = J // 2
 RUN = 2
+WHOLE = 0
 
 
 def plane(table, t):
@@ -67,33 +68,30 @@ def tile_picked_largercode_respelled_one_codedgain_store_plain_kernel(
         ua_sb.append(load_plane(ua, 1, "ua"))
         l4 = load_list(offs4, "l4")
         hb_early = load_factors(nc.sync, by_plane(hb)[:, 0:2], "hb_early")
-        ga_sb = load_factors(nc.sync, by_plane(ga), "ga_sb")
-        gb_sb = load_factors(nc.sync, by_plane(gb), "gb_sb")
         ua_sb.append(load_plane(ua, 2, "ua"))
+        scale_rows = sb.tile([P, S], U8, name="scale_rows")
+        nc.vector.memset(scale_rows[:].bitcast(I32), 0)
+        for q in range(4):
+            nc.sync.dma_start(
+                scale_rows[32 * q : 32 * q + 4, :].bitcast(I32),
+                vs_scales[0, 4 * q : 4 * q + 4, :].bitcast(I32),
+            )
         ua_sb.append(load_plane(ua, 3, "ua"))
         hb_late = load_factors(nc.sync, by_plane(hb)[:, 2:4], "hb_late")
         l7 = load_list(offs7, "l7")
         words = sb.tile([P, 2 * S], U8, name="words")
         nc.sync.dma_start(words[:].bitcast(I32), vs_words[0].bitcast(I32))
-        ta_sb, tb_sb = [], []
-        for t in range(PACK):
-            ta_sb.append(load_plane(ta, t, "ta"))
-            tb_sb.append(load_plane(tb, t, "tb"))
         l1 = load_list(offs, "l1")
+        ga_sb = load_factors(nc.sync, by_plane(ga), "ga_sb")
+        ta_sb = [load_plane(ta, t, "ta") for t in range(PACK)]
+        gb_sb = load_factors(nc.sync, by_plane(gb), "gb_sb")
+        tb_sb = [load_plane(tb, t, "tb") for t in range(PACK)]
         l2 = load_list(offs2, "l2")
         l6 = load_list(offs6, "l6")
+        sl_sb = load_factors(nc.sync, by_plane(sl), "sl_sb")
         tl_sb = [load_plane(tl, t, "tl") for t in range(PACK)]
         l5 = load_list(offs5, "l5")
-
-        sl_sb = load_factors(nc.gpsimd, by_plane(sl), "sl_sb")
-        sa_sb = load_factors(nc.gpsimd, by_plane(sa), "sa_sb")
-        scale_rows = sb.tile([P, S], U8, name="scale_rows")
-        nc.vector.memset(scale_rows[:].bitcast(I32), 0)
-        for q in range(4):
-            nc.gpsimd.dma_start(
-                scale_rows[32 * q : 32 * q + 4, :].bitcast(I32),
-                vs_scales[0, 4 * q : 4 * q + 4, :].bitcast(I32),
-            )
+        sa_sb = load_factors(nc.sync, by_plane(sa), "sa_sb")
 
         wc = sb.tile([P, PACK, R], BF16, name="wc")
         for pair, hb_sb in enumerate((hb_early, hb_late)):
@@ -124,18 +122,22 @@ def tile_picked_largercode_respelled_one_codedgain_store_plain_kernel(
         a_sb = [sb.tile([P, J], F32, name="a%d" % s) for s in range(PACK)]
         first_bank = ps.tile([P, PACK, HALF], F32, name="first_bank")
         sums = []
+        xa = sb.tile([P, PACK, J], F32, name="xa")
+        xb = sb.tile([P, PACK, J], F32, name="xb")
+        for t in range(PACK):
+            gather_scaled(xa[:, t, :], ta_sb[t], l1[:], ga_sb[:, t : t + 1])
+        for t in range(WHOLE):
+            gather_scaled(xb[:, t, :], tb_sb[t], l2[:], gb_sb[:, t : t + 1])
         for h in range(2):
+            slots = slice(h * HALF, (h + 1) * HALF)
             cols = slice(h * HALF // 16, (h + 1) * HALF // 16)
-            xa = sb.tile([P, PACK, HALF], F32, name="xa%d" % h)
-            xb = sb.tile([P, PACK, HALF], F32, name="xb%d" % h)
-            for t in range(PACK):
-                gather_scaled(xa[:, t, :], ta_sb[t], l1[:, cols], ga_sb[:, t : t + 1])
-                gather_scaled(xb[:, t, :], tb_sb[t], l2[:, cols], gb_sb[:, t : t + 1])
-            xc_grouped = sb.tile([P, HALF, PACK], BF16, name="xc_grouped%d" % h, align_bytes=64)
+            for t in range(WHOLE, PACK):
+                gather_scaled(xb[:, t, slots], tb_sb[t], l2[:, cols], gb_sb[:, t : t + 1])
+            xc_grouped = sb.tile([P, HALF, PACK], BF16, name="xc_grouped", align_bytes=64)
             nc.vector.tensor_tensor(
                 out=xc_grouped[:].rearrange("p (c i) t -> p c t i", i=RUN),
-                in0=xa[:].rearrange("p t (c i) -> p c t i", i=RUN),
-                in1=xb[:].rearrange("p t (c i) -> p c t i", i=RUN),
+                in0=xa[:, :, slots].rearrange("p t (c i) -> p c t i", i=RUN),
+                in1=xb[:, :, slots].rearrange("p t (c i) -> p c t i", i=RUN),
                 op=ALU.max,
             )
             xc_codes = sb.tile([P, HALF], U32, name="xc_codes%d" % h, align_bytes=64)
@@ -165,21 +167,31 @@ def tile_picked_largercode_respelled_one_codedgain_store_plain_kernel(
         picked = sb.tile([P, PACK, O], F32, name="picked")
         for s in range(PACK):
             gather_scaled(gain[:, s, :], tl_sb[s], l6[:], sl_sb[:, s : s + 1])
-        for s in range(PACK):
+        for s in range(PACK - 1):
             gather_scaled(picked[:, s, :], a_sb[s], l5[:], sa_sb[:, s : s + 1])
-        hid_grouped = sb.tile([P, O, PACK], BF16, name="hid_grouped", align_bytes=64)
-        nc.vector.tensor_tensor(
-            out=hid_grouped[:].rearrange("p (c i) s -> p c s i", i=RUN),
-            in0=picked[:].rearrange("p s (c i) -> p c s i", i=RUN),
-            in1=gain[:].rearrange("p s (c i) -> p c s i", i=RUN),
-            op=ALU.mult,
-        )
+        for h in range(2):
+            gather_scaled(
+                picked[:, PACK - 1, h * O // 2 : (h + 1) * O // 2], a_sb[PACK - 1],
+                l5[:, h * O // 32 : (h + 1) * O // 32], sa_sb[:, PACK - 1 : PACK],
+            )
         hid_codes = sb.tile([P, O], U32, name="hid_codes", align_bytes=64)
         hid_scales = sb.tile([P, O], U8, name="hid_scales", align_bytes=64)
-        nc.vector.quantize_mx(
-            out=hid_codes[:].bitcast(FP8X4), scales=hid_scales[:],
-            in_=hid_grouped[:].rearrange("p o s -> p (o s)"),
-        )
+        hid_grouped = []
+        for h in range(2):
+            places = slice(h * O // 2, (h + 1) * O // 2)
+            hid_grouped.append(sb.tile([P, O // 2, PACK], BF16, name="hid_grouped%d" % h, align_bytes=64))
+            nc.vector.tensor_tensor(
+                out=hid_grouped[h][:].rearrange("p (c i) s -> p c s i", i=RUN),
+                in0=picked[:, :, places].rearrange("p s (c i) -> p c s i", i=RUN),
+                in1=gain[:, :, places].rearrange("p s (c i) -> p c s i", i=RUN),
+                op=ALU.mult,
+            )
+        for h in range(2):
+            places = slice(h * O // 2, (h + 1) * O // 2)
+            nc.vector.quantize_mx(
+                out=hid_codes[:, places].bitcast(FP8X4), scales=hid_scales[:, places],
+                in_=hid_grouped[h][:].rearrange("p o s -> p (o s)"),
+            )
 
         for b in range(N // P):
             y_bank = ps.tile([P, O], F32, name="y_bank%d" % b)

from contextlib import ExitStack

import concourse.mybir as mybir

K, J, R, T, U, F, G, O, D, N, S = 512, 256, 512, 512, 512, 2048, 1024, 128, 512, 256, 1024
FLOPS = 2 * K * R * J + 2 * R * N * O

F32 = mybir.dt.float32
BF16 = mybir.dt.bfloat16
I32 = mybir.dt.int32
U32 = mybir.dt.uint32
U16 = mybir.dt.uint16
U8 = mybir.dt.uint8
FP8X4 = mybir.dt.float8_e4m3fn_x4
FP4X4 = mybir.dt.float4_e2m1fn_x4
COPY = mybir.ActivationFunctionType.Copy
ALU = mybir.AluOpType

P = 128
PACK = 4
HALF = J // 2
RUN = 2
WHOLE = 0


def plane(table, t):
    return table.rearrange("(p t) c -> p t c", t=PACK)[:, t, :]


def by_plane(column):
    return column.rearrange("(p t) one -> p (t one)", t=PACK)


def tile_picked_largercode_respelled_one_codedgain_store_plain_kernel(
    tc, ta, tb, ga, gb, ua, ha, hb, tl, sa, sl, vs_words, vs_scales,
    offs, offs2, offs3, offs4, offs5, offs6, offs7, out,
):
    nc = tc.nc
    with ExitStack() as ctx:
        sb = ctx.enter_context(tc.tile_pool(name="sb", bufs=1))
        ps = ctx.enter_context(tc.psum_pool(name="ps", bufs=1))

        def load_list(src, name):
            dst = sb.tile(list(src.shape), U16, name=name)
            nc.sync.dma_start(dst[:], src)
            return dst

        def load_plane(table, t, name):
            dst = sb.tile([P, table.shape[1]], F32, name="%s%d" % (name, t))
            nc.sync.dma_start(dst[:], plane(table, t))
            return dst

        def load_factors(engine, src, name):
            dst = sb.tile(list(src.shape), F32, name=name)
            engine.dma_start(dst[:], src)
            return dst

        def gather_scaled(dst, window, offsets, factor):
            nc.scalar.activation(out=dst, in_=window[:].indirect(offsets), func=COPY, scale=factor)

        ha_sb = load_factors(nc.scalar, by_plane(ha), "ha_sb")
        warm_in = sb.tile([P, 1], F32, name="warm_in")
        warm_out = sb.tile([P, 1], F32, name="warm_out")
        nc.vector.memset(warm_in[:], 0.0)
        nc.scalar.activation(out=warm_out[:], in_=warm_in[:], func=COPY)
        ua_sb = [load_plane(ua, 0, "ua")]
        l3 = load_list(offs3, "l3")
        ua_sb.append(load_plane(ua, 1, "ua"))
        l4 = load_list(offs4, "l4")
        hb_early = load_factors(nc.sync, by_plane(hb)[:, 0:2], "hb_early")
        ua_sb.append(load_plane(ua, 2, "ua"))
        scale_rows = sb.tile([P, S], U8, name="scale_rows")
        nc.vector.memset(scale_rows[:].bitcast(I32), 0)
        for q in range(4):
            nc.sync.dma_start(
                scale_rows[32 * q : 32 * q + 4, :].bitcast(I32),
                vs_scales[0, 4 * q : 4 * q + 4, :].bitcast(I32),
            )
        ua_sb.append(load_plane(ua, 3, "ua"))
        hb_late = load_factors(nc.sync, by_plane(hb)[:, 2:4], "hb_late")
        l7 = load_list(offs7, "l7")
        words = sb.tile([P, 2 * S], U8, name="words")
        nc.sync.dma_start(words[:].bitcast(I32), vs_words[0].bitcast(I32))
        l1 = load_list(offs, "l1")
        ga_sb = load_factors(nc.sync, by_plane(ga), "ga_sb")
        ta_sb = [load_plane(ta, t, "ta") for t in range(PACK)]
        gb_sb = load_factors(nc.sync, by_plane(gb), "gb_sb")
        tb_sb = [load_plane(tb, t, "tb") for t in range(PACK)]
        l2 = load_list(offs2, "l2")
        l6 = load_list(offs6, "l6")
        sl_sb = load_factors(nc.sync, by_plane(sl), "sl_sb")
        tl_sb = [load_plane(tl, t, "tl") for t in range(PACK)]
        l5 = load_list(offs5, "l5")
        sa_sb = load_factors(nc.sync, by_plane(sa), "sa_sb")

        wc = sb.tile([P, PACK, R], BF16, name="wc")
        for pair, hb_sb in enumerate((hb_early, hb_late)):
            wcd = []
            for u in range(2):
                t = 2 * pair + u
                wcd.append(sb.tile([P, G], F32, name="wcd%d" % t))
                gather_scaled(wcd[u][:], ua_sb[t], l3[:], ha_sb[:, t : t + 1])
            for u in range(2):
                gather_scaled(wc[:, 2 * pair + u, :], wcd[u], l4[:], hb_sb[:, u : u + 1])
        wc_grouped = sb.tile([P, R, PACK], BF16, name="wc_grouped", align_bytes=64)
        nc.vector.tensor_copy(
            out=wc_grouped[:].rearrange("p (s m) t -> p s m t", s=PACK),
            in_=wc[:].rearrange("p t (m s) -> p s m t", s=PACK),
        )
        wc_codes = sb.tile([P, R], U32, name="wc_codes", align_bytes=64)
        wc_scales = sb.tile([P, R], U8, name="wc_scales", align_bytes=64)
        nc.vector.quantize_mx(
            out=wc_codes[:].bitcast(FP8X4), scales=wc_scales[:],
            in_=wc_grouped[:].rearrange("p r t -> p (r t)"),
        )

        vs_codes = sb.tile([P, 2 * N], U8, name="vs_codes", align_bytes=64)
        vs_bytes = sb.tile([P, N], U8, name="vs_bytes", align_bytes=64)
        nc.vector.tensor_copy(out=vs_codes[:].bitcast(U16), in_=words[:].bitcast(U16).indirect(l7[:]))
        nc.vector.tensor_copy(out=vs_bytes[:], in_=scale_rows[:].indirect(l7[:]))

        a_sb = [sb.tile([P, J], F32, name="a%d" % s) for s in range(PACK)]
        first_bank = ps.tile([P, PACK, HALF], F32, name="first_bank")
        sums = []
        xa = sb.tile([P, PACK, J], F32, name="xa")
        xb = sb.tile([P, PACK, J], F32, name="xb")
        for t in range(PACK):
            gather_scaled(xa[:, t, :], ta_sb[t], l1[:], ga_sb[:, t : t + 1])
        for t in range(WHOLE):
            gather_scaled(xb[:, t, :], tb_sb[t], l2[:], gb_sb[:, t : t + 1])
        for h in range(2):
            slots = slice(h * HALF, (h + 1) * HALF)
            cols = slice(h * HALF // 16, (h + 1) * HALF // 16)
            for t in range(WHOLE, PACK):
                gather_scaled(xb[:, t, slots], tb_sb[t], l2[:, cols], gb_sb[:, t : t + 1])
            xc_grouped = sb.tile([P, HALF, PACK], BF16, name="xc_grouped", align_bytes=64)
            nc.vector.tensor_tensor(
                out=xc_grouped[:].rearrange("p (c i) t -> p c t i", i=RUN),
                in0=xa[:, :, slots].rearrange("p t (c i) -> p c t i", i=RUN),
                in1=xb[:, :, slots].rearrange("p t (c i) -> p c t i", i=RUN),
                op=ALU.max,
            )
            xc_codes = sb.tile([P, HALF], U32, name="xc_codes%d" % h, align_bytes=64)
            xc_scales = sb.tile([P, HALF], U8, name="xc_scales%d" % h, align_bytes=64)
            nc.vector.quantize_mx(
                out=xc_codes[:].bitcast(FP8X4), scales=xc_scales[:],
                in_=xc_grouped[:].rearrange("p j t -> p (j t)"),
            )
            for s in range(PACK):
                if h == 0:
                    acc = first_bank[:, s, :]
                else:
                    bank = ps.tile([P, HALF], F32, name="bank%d" % s)
                    acc = bank[:]
                rows = slice(s * P, (s + 1) * P)
                nc.tensor.matmul_mx(
                    out=acc,
                    lhsT=wc_codes[:, rows].bitcast(FP8X4), lhsT_scale=wc_scales[:, rows],
                    rhs=xc_codes[:].bitcast(FP8X4), rhs_scale=xc_scales[:],
                    start=True, stop=True,
                )
                sums.append((a_sb[s][:, h * HALF : (h + 1) * HALF], acc))
        for dst, acc in sums:
            nc.vector.tensor_copy(out=dst, in_=acc)

        gain = sb.tile([P, PACK, O], F32, name="gain")
        picked = sb.tile([P, PACK, O], F32, name="picked")
        for s in range(PACK):
            gather_scaled(gain[:, s, :], tl_sb[s], l6[:], sl_sb[:, s : s + 1])
        for s in range(PACK - 1):
            gather_scaled(picked[:, s, :], a_sb[s], l5[:], sa_sb[:, s : s + 1])
        for h in range(2):
            gather_scaled(
                picked[:, PACK - 1, h * O // 2 : (h + 1) * O // 2], a_sb[PACK - 1],
                l5[:, h * O // 32 : (h + 1) * O // 32], sa_sb[:, PACK - 1 : PACK],
            )
        hid_codes = sb.tile([P, O], U32, name="hid_codes", align_bytes=64)
        hid_scales = sb.tile([P, O], U8, name="hid_scales", align_bytes=64)
        hid_grouped = []
        for h in range(2):
            places = slice(h * O // 2, (h + 1) * O // 2)
            hid_grouped.append(sb.tile([P, O // 2, PACK], BF16, name="hid_grouped%d" % h, align_bytes=64))
            nc.vector.tensor_tensor(
                out=hid_grouped[h][:].rearrange("p (c i) s -> p c s i", i=RUN),
                in0=picked[:, :, places].rearrange("p s (c i) -> p c s i", i=RUN),
                in1=gain[:, :, places].rearrange("p s (c i) -> p c s i", i=RUN),
                op=ALU.mult,
            )
        for h in range(2):
            places = slice(h * O // 2, (h + 1) * O // 2)
            nc.vector.quantize_mx(
                out=hid_codes[:, places].bitcast(FP8X4), scales=hid_scales[:, places],
                in_=hid_grouped[h][:].rearrange("p o s -> p (o s)"),
            )

        for b in range(N // P):
            y_bank = ps.tile([P, O], F32, name="y_bank%d" % b)
            nc.tensor.matmul_mx(
                out=y_bank[:],
                lhsT=vs_codes[:, 2 * P * b : 2 * P * (b + 1)].bitcast(FP4X4),
                lhsT_scale=vs_bytes[:, P * b : P * (b + 1)],
                rhs=hid_codes[:].bitcast(FP8X4), rhs_scale=hid_scales[:],
                start=True, stop=True,
            )
            y_sb = sb.tile([P, O], F32, name="y_sb%d" % b)
            if b == 0:
                nc.vector.tensor_copy(out=y_sb[:], in_=y_bank[:])
                nc.sync.dma_start(out[0:P, :], y_sb[:])
            else:
                nc.scalar.copy(out=y_sb[:], in_=y_bank[:])
                nc.scalar.dma_start(out[P : 2 * P, :], y_sb[:])
